import numpy as np
import ml_dtypes


def mxq(x, axis, fmt="e4m3"):
    dtype, down = {"e4m3": (ml_dtypes.float8_e4m3fn, 7), "e5m2": (ml_dtypes.float8_e5m2, 14)}[fmt]
    v = np.moveaxis(np.asarray(x, np.float32).astype(ml_dtypes.bfloat16).astype(np.float64), axis, -1)
    blocks = v.reshape(v.shape[:-1] + (-1, 32))
    amax = np.abs(blocks).max(-1, keepdims=True)
    byte = np.maximum(np.where(amax > 0, np.frexp(amax)[1] - 1 + 127, 0) - down, 1)
    scale = np.exp2(byte - 127.0)
    codes = (blocks / scale).astype(np.float32).astype(dtype).astype(np.float64)
    return np.moveaxis((codes * scale).reshape(v.shape), -1, axis)


WIDE = False


def mx_kscale(k):
    if not WIDE:
        return np.ones(k)
    levels = np.array([10, -10, 5, -5, 0])
    if k % 512:
        return np.exp2(np.random.permutation(np.resize(levels, k // 32))).repeat(32)
    a = np.empty((k // 512, 16))
    for p in range(k // 512):
        a[p, :8] = np.random.permutation(np.resize(levels, 8))
        for g in range(8):
            far = levels[np.abs(levels - a[p, g]) >= 10]
            a[p, g + 8] = far[np.random.randint(len(far))]
    return np.exp2(a.ravel()).repeat(32)


def f64(x):
    return np.asarray(x).astype(np.float64)


def striped(idx):
    return np.tile(np.asarray(idx).reshape(-1, 16).T, (8, 1)).astype(np.uint16)


def unstriped(offs):
    return offs[:16].T.reshape(-1).astype(np.int64)


E2M1 = np.array([0.0, 0.5, 1.0, 1.5, 2.0, 3.0, 4.0, 6.0, -0.0, -0.5, -1.0, -1.5, -2.0, -3.0, -4.0, -6.0])


def pack_weight(w, fmt):
    k, n = w.shape
    w = f64(np.asarray(w, np.float32).astype(ml_dtypes.bfloat16)).reshape(k // 32, 32, n)
    amax = np.abs(w).max(1)
    if fmt == "e4m3":
        byte = np.frexp(amax)[1] - 1 + 127 - 7
    else:
        mant, ex = np.frexp(amax / 6.0)
        byte = np.where(mant > 0.5, ex, ex - 1) + 127
    byte = np.clip(np.where(amax > 0, byte, 1), 1, 254)
    scaled = (w * np.exp2(127.0 - byte)[:, None, :]).reshape(k, n).astype(np.float32)
    by_word = np.ascontiguousarray(scaled.reshape(k // 512, 128, 4, n).transpose(0, 1, 3, 2))
    if fmt == "e4m3":
        words = by_word.astype(ml_dtypes.float8_e4m3fn).view(np.uint8)
    else:
        c = by_word.astype(ml_dtypes.float4_e2m1fn).view(np.uint8) & 0xF
        words = (c[..., 0::2] | (c[..., 1::2] << 4)).reshape(k // 512, 128, 2 * n)
    return np.ascontiguousarray(words), np.ascontiguousarray(byte.astype(np.uint8).reshape(k // 512, 16, n))


def unpack_weight(words, scales, fmt):
    g, _, n = scales.shape
    words = np.ascontiguousarray(words).reshape(g, 128, n, -1)
    if fmt == "e4m3":
        vals = words.view(ml_dtypes.float8_e4m3fn).astype(np.float64)
    else:
        nib = np.empty((g, 128, n, 4), np.uint8)
        nib[..., 0::2] = words & 0xF
        nib[..., 1::2] = words >> 4
        vals = E2M1[nib]
    vals = vals * np.repeat(np.exp2(scales.astype(np.float64) - 127.0), 8, axis=1)[..., None]
    return vals.transpose(0, 1, 3, 2).reshape(g * 512, n)


def sigmoid(v):
    return 1.0 / (1.0 + np.exp(-v))


D, K, R, T, I, Q, G = 512, 512, 512, 1024, 256, 512, 16


def setup_inputs():
    n = np.random.standard_normal
    idx = np.random.permutation(T)[:I]
    fd = mx_kscale(D)
    fk = mx_kscale(K)
    fq = mx_kscale(Q)
    keysp = pack_weight(n((D, T)) / fd[:, None], "e2m1")
    tabp = pack_weight(n((K, T)) / fk[:, None], "e2m1")
    return {
        "query": (n((D, Q)) * 0.6 / np.sqrt(D) * fd[:, None]).astype(np.float32),
        "query2": (n((D, Q)) * 1.0 / np.sqrt(D) * fd[:, None]).astype(np.float32),
        "keys_words": keysp[0],
        "keys_scales": keysp[1],
        "tab_words": tabp[0],
        "tab_scales": tabp[1],
        "w1": (n((K, R)) * 1 / np.sqrt(K) * fk[:, None]).astype(np.float32),
        "share": (np.random.uniform(0.4, 1.0, (R, 1))).astype(np.float32),
        "qs": (np.random.uniform(4.0, 16.0, (Q, 1)) * fq[:, None]).astype(np.float32),
        "grows": (n((Q, R)) / fq[:, None]).astype(np.float32),
        "sg": (np.random.uniform(0.5, 2.0, (1, I))).astype(np.float32),
        "old": (0.4 * n((R, I))).astype(np.float32),
        "offs": striped(idx),
    }


def reference(query, query2, keys_words, keys_scales, tab_words, tab_scales, w1, share, qs, grows, sg, old, offs):
    idx = unstriped(offs)
    keysu = unpack_weight(keys_words, keys_scales, "e2m1")
    tabu = unpack_weight(tab_words, tab_scales, "e2m1")
    queryq = mxq(f64(query), 0, "e4m3")
    keysidxg = keysu[:, idx]
    a = queryq.T @ keysidxg
    query2q = mxq(f64(query2), 0, "e4m3")
    b = query2q.T @ keysidxg
    p = np.exp(a - np.max(a, axis=1, keepdims=True)) * sigmoid(b)
    z = np.sum(p, axis=1, keepdims=True)
    w = p / z
    wq = w * f64(qs)
    w1q = mxq(f64(w1), 0, "e4m3")
    tabidxg = tabu[:, idx]
    zh = w1q.T @ tabidxg
    mz = zh.reshape(R, G, I // G).mean(axis=2)
    mzr = np.repeat(mz, I // G, axis=1)
    hv = np.tanh(zh - mzr * f64(share))
    growsq = mxq(f64(grows), 0, "e4m3")
    wqq = mxq(wq, 0, "e4m3")
    c0 = growsq.T @ wqq
    dmzr = c0 * (1.0 - np.square(hv)) * (-1.0) * f64(share)
    dmz = dmzr.reshape(R, G, I // G).sum(axis=2)
    e1 = dmz / 16.0
    r1 = np.repeat(e1, I // G, axis=1)
    dzh = c0 * (1.0 - np.square(hv)) + r1
    y = dzh * f64(sg) + f64(old)
    return y

@@ -1,0 +1,208 @@
+from contextlib import ExitStack
+
+import concourse.mybir as mybir
+from concourse.masks import make_identity
+
+F32 = mybir.dt.float32
+BF16 = mybir.dt.bfloat16
+I32 = mybir.dt.int32
+U32 = mybir.dt.uint32
+U16 = mybir.dt.uint16
+U8 = mybir.dt.uint8
+FP8X4 = mybir.dt.float8_e4m3fn_x4
+FP4X4 = mybir.dt.float4_e2m1fn_x4
+ALU = mybir.AluOpType
+ACT = mybir.ActivationFunctionType
+AX = mybir.AxisListType
+
+P = 128
+PACK = 4
+WIDTH = 512
+POOL = 1024
+SLOTS = 256
+PAGE = 16
+PAGES = SLOTS // PAGE
+
+FLOPS = 4 * 2 * 512 * 512 * SLOTS
+
+
+def tile_attend_bzcentred_asked_kernel(tc, query, query2, keys_words, keys_scales, tab_words, tab_scales,
+                                        w1, share, qs, grows, sg, old, offs, out):
+    nc = tc.nc
+    with ExitStack() as ctx:
+        sb = ctx.enter_context(tc.tile_pool(name="sb", bufs=1))
+        ps = ctx.enter_context(tc.psum_pool(name="ps", bufs=1))
+
+        def tile(name, shape, dtype):
+            return sb.tile(shape, dtype, name=name, align_bytes=64)
+
+        def banks(name, tag):
+            return [ps.tile([P, 2, SLOTS], F32, name=name + str(h), tag=tag + str(h)) for h in range(2)]
+
+        offsets = sb.tile([P, SLOTS // 16], U16, name="offsets")
+        key_bytes = tile("key_bytes", [P, POOL], U8)
+        tab_bytes = tile("tab_bytes", [P, POOL], U8)
+        nc.vector.memset(tab_bytes[:].bitcast(I32), 0)
+        nc.gpsimd.memset(key_bytes[:].bitcast(I32), 0)
+        nc.sync.dma_start(offsets[:], offs)
+
+        def load(name, src):
+            raw = tile(name, [P, PACK, WIDTH], F32)
+            nc.sync.dma_start(raw[:], src.rearrange("(p t) c -> p t c", t=PACK))
+            return raw
+
+        def load_bytes(dst, src):
+            for quad in range(4):
+                nc.sync.dma_start(dst[32 * quad:32 * quad + 4, :].bitcast(I32),
+                                  src[0, 4 * quad:4 * quad + 4, :].bitcast(I32))
+
+        tab_pool = tile("tab_pool", [P, POOL], U16)
+        nc.sync.dma_start(tab_pool[:].bitcast(I32), tab_words[0].bitcast(I32))
+        load_bytes(tab_bytes, tab_scales)
+        w1_raw = load("w1_raw", w1)
+        key_words = tile("key_words", [P, POOL], U16)
+        nc.sync.dma_start(key_words[:].bitcast(I32), keys_words[0].bitcast(I32))
+        load_bytes(key_bytes, keys_scales)
+        q2_raw = load("q2_raw", query2)
+        q_raw = load("q_raw", query)
+        share_sb = tile("share_sb", [P, PACK], F32)
+        nc.sync.dma_start(share_sb[:], share.rearrange("(p j) o -> p (j o)", j=PACK))
+        qs_sb = tile("qs_sb", [P, PACK], F32)
+        nc.sync.dma_start(qs_sb[:], qs.rearrange("(p j) o -> p (j o)", j=PACK))
+        sg_col = tile("sg_col", [P, 2], F32)
+        nc.sync.dma_start(sg_col[:], sg.rearrange("o (p e) -> p (o e)", e=2))
+        g_raw = load("g_raw", grows)
+        old_sb = tile("old_sb", [P, PACK, SLOTS], F32)
+        nc.sync.dma_start(old_sb[:], old.rearrange("(p j) i -> p j i", j=PACK))
+        ident = tile("ident", [P, P], F32)
+        make_identity(nc, ident[:])
+        share16 = tile("share16", [P, PACK], F32)
+        nc.gpsimd.tensor_scalar(share16[:], share_sb[:], 1.0 / PAGE, 0.0, ALU.mult, ALU.add)
+        warm2 = tile("warm2", [P, 1], F32)
+        nc.scalar.activation(warm2[:], ident[:, 0:1], ACT.Sigmoid)
+        def gather(name, window, dtype):
+            got = tile(name, [P, SLOTS], dtype)
+            nc.vector.tensor_copy(got[:], window[:].indirect(offsets[:]))
+            return got
+
+        def deal(name, raw, shares):
+            dealt = tile(name, [P, PACK, P, PACK], BF16)
+            dst = dealt[:].rearrange("p r s t -> p s t r")
+            src = raw[:].rearrange("p t (s r) -> p s t r", r=PACK)
+            lo = 0
+            for engine, cols in shares:
+                part = slice(lo, lo + cols)
+                if engine == "v":
+                    nc.vector.tensor_copy(dst[:, part], src[:, part])
+                elif engine == "s":
+                    nc.scalar.copy(dst[:, part], src[:, part])
+                else:
+                    nc.gpsimd.tensor_scalar(dst[:, part], src[:, part], 1.0, 0.0, ALU.mult, ALU.add)
+                lo = lo + cols
+            return dealt[:].rearrange("p r s t -> p (r s t)")
+
+        def quantize(name, values, width):
+            codes = tile(name + "_codes", [P, width], U32)
+            scales = tile(name + "_scales", [P, width], U8)
+            nc.vector.quantize_mx(out=codes[:].bitcast(FP8X4), scales=scales[:], in_=values)
+            return codes, scales
+
+        def product(dst, stationary, moving_codes, moving_scales):
+            codes, scales = stationary
+            for r in range(PACK):
+                cols = slice(P * r, P * (r + 1))
+                nc.tensor.matmul_mx(out=dst[r // 2][:, r % 2, :], lhsT=codes[:, cols].bitcast(FP8X4),
+                                    lhsT_scale=scales[:, cols], rhs=moving_codes, rhs_scale=moving_scales,
+                                    start=True, stop=True)
+
+        def paged(ap):
+            return ap.rearrange("p (g m) -> p g m", m=PAGE)
+
+        def spread(sums):
+            return sums.unsqueeze(2).to_broadcast([P, PAGES, PAGE])
+
+        tabs = gather("tabs", tab_pool, U16)
+        tab_scale = gather("tab_scale", tab_bytes, U8)
+        w1_bf = deal("w1_bf", w1_raw, [("v", 72), ("s", 56)])
+        keys = gather("keys", key_words, U16)
+        w1_mx = quantize("w1", w1_bf, WIDTH)
+        z_ps = banks("z_ps", "layer")
+        product(z_ps, w1_mx, tabs[:].bitcast(FP4X4), tab_scale[:])
+        key_scale = gather("key_scale", key_bytes, U8)
+        q2_bf = deal("q2_bf", q2_raw, [("v", 72), ("s", 56)])
+        q2_mx = quantize("q2", q2_bf, WIDTH)
+        b_ps = banks("b_ps", "early")
+        product(b_ps, q2_mx, keys[:].bitcast(FP4X4), key_scale[:])
+        gate = tile("gate", [P, PACK, SLOTS], F32)
+        for h in range(2):
+            nc.scalar.activation(gate[:, 2 * h:2 * h + 2, :], b_ps[h][:], ACT.Sigmoid)
+        z_sum = tile("z_sum", [P, PACK, PAGES], F32)
+        for h in range(2):
+            nc.vector.tensor_reduce(z_sum[:, 2 * h:2 * h + 2, :],
+                                    z_ps[h][:].rearrange("p j (g m) -> p j g m", m=PAGE), AX.X, ALU.add)
+        q_bf = deal("q_bf", q_raw, [("v", 128)])
+        q_mx = quantize("q", q_bf, WIDTH)
+        a_ps = banks("a_ps", "score")
+        product(a_ps, q_mx, keys[:].bitcast(FP4X4), key_scale[:])
+        sg_ps = ps.tile([P, 2, P], F32, name="sg_ps", tag="sg")
+        for e in range(2):
+            nc.tensor.transpose(sg_ps[:, e, :], sg_col[:, e:e + 1].to_broadcast([P, P]), ident[:])
+
+        centred = tile("centred", [P, PACK, SLOTS], F32)
+        for j in range(PACK):
+            nc.vector.scalar_tensor_tensor(paged(centred[:, j, :]), spread(z_sum[:, j, :]), share16[:, j:j + 1],
+                                           paged(z_ps[j // 2][:, j % 2, :]), ALU.mult, ALU.subtract)
+        neg_max = tile("neg_max", [P, PACK], F32)
+        for h in range(2):
+            nc.vector.tensor_reduce(neg_max[:, 2 * h:2 * h + 2], a_ps[h][:], AX.X, ALU.max, negate=True)
+        expo = tile("expo", [P, PACK, SLOTS], F32)
+        for t in range(PACK):
+            nc.scalar.activation(expo[:, t, :], a_ps[t // 2][:, t % 2, :], ACT.Exp, bias=neg_max[:, t:t + 1])
+        g_bf = deal("g_bf", g_raw, [("s", 32), ("s", 32), ("s", 32), ("s", 32)])
+        prob = tile("prob", [P, PACK, SLOTS], F32)
+        row_sum = tile("row_sum", [P, PACK], F32)
+        for t in range(PACK):
+            nc.vector.scalar_tensor_tensor(prob[:, t, :], expo[:, t, :], 1.0, gate[:, t, :], ALU.mult, ALU.mult,
+                                           accum_out=row_sum[:, t:t + 1])
+        inv_sum = tile("inv_sum", [P, PACK], F32)
+        nc.vector.reciprocal(inv_sum[:], row_sum[:])
+        g_mx = quantize("g", g_bf, WIDTH)
+        factor = tile("factor", [P, PACK], F32)
+        nc.vector.tensor_tensor(factor[:], inv_sum[:], qs_sb[:], ALU.mult)
+        hv = tile("hv", [P, PACK, SLOTS], F32)
+        hv2 = tile("hv2", [P, PACK, SLOTS], F32)
+        for h in range(2):
+            nc.scalar.activation(hv[:, 2 * h:2 * h + 2, :], centred[:, 2 * h:2 * h + 2, :], ACT.Tanh)
+            nc.scalar.activation(hv2[:, 2 * h:2 * h + 2, :], hv[:, 2 * h:2 * h + 2, :], ACT.Square)
+        wq_bf = tile("wq_bf", [P, SLOTS, PACK], BF16)
+        nc.vector.tensor_tensor(
+            wq_bf[:].rearrange("p (c i) t -> p c t i", i=4),
+            prob[:].rearrange("p t (c i) -> p c t i", i=4),
+            factor[:].unsqueeze(1).unsqueeze(3).to_broadcast([P, SLOTS // 4, PACK, 4]), ALU.mult)
+        wq_codes, wq_scales = quantize("wq", wq_bf[:].rearrange("p i t -> p (i t)"), SLOTS)
+        c_ps = banks("c_ps", "early")
+        product(c_ps, g_mx, wq_codes[:].bitcast(FP8X4), wq_scales[:])
+        neg_g = tile("neg_g", [P, PACK, SLOTS], F32)
+        g_sum = tile("g_sum", [P, PACK, PAGES], F32)
+        dzh = tile("dzh", [P, PACK, SLOTS], F32)
+        gained = tile("gained", [P, PACK, SLOTS], F32)
+        result = tile("result", [P, PACK, SLOTS], F32)
+        out_v = out.rearrange("(p j) i -> p j i", j=PACK)
+        for h in range(2):
+            pair = slice(2 * h, 2 * h + 2)
+            nc.vector.scalar_tensor_tensor(neg_g[:, pair, :], hv2[:, pair, :], 1.0, c_ps[h][:], ALU.subtract, ALU.mult)
+        for h in range(2):
+            pair = slice(2 * h, 2 * h + 2)
+            nc.vector.tensor_reduce(g_sum[:, pair, :], neg_g[:, pair, :].rearrange("p j (g m) -> p j g m", m=PAGE),
+                                    AX.X, ALU.add)
+        for h in range(2):
+            pair = slice(2 * h, 2 * h + 2)
+            for j in range(2 * h, 2 * h + 2):
+                nc.vector.scalar_tensor_tensor(paged(dzh[:, j, :]), spread(g_sum[:, j, :]), share16[:, j:j + 1],
+                                               paged(neg_g[:, j, :]), ALU.mult, ALU.subtract)
+            nc.vector.tensor_tensor(
+                gained[:, pair, :].rearrange("p j (k e) -> p j k e", e=2),
+                dzh[:, pair, :].rearrange("p j (k e) -> p j k e", e=2),
+                sg_ps[:].rearrange("p e k -> p k e").unsqueeze(1).to_broadcast([P, 2, P, 2]), ALU.mult)
+            (nc.gpsimd if h == 0 else nc.vector).tensor_tensor(result[:, pair, :], gained[:, pair, :], old_sb[:, pair, :], ALU.add)
+            nc.sync.dma_start(out_v[:, pair, :], result[:, pair, :])

@@ -33,8 +33,8 @@ def tile_attend_bzcentred_asked_kernel(tc, query, query2, keys_words, keys_scale
         sb = ctx.enter_context(tc.tile_pool(name="sb", bufs=1))
         ps = ctx.enter_context(tc.psum_pool(name="ps", bufs=1))
 
-        def tile(name, shape, dtype):
-            return sb.tile(shape, dtype, name=name, align_bytes=64)
+        def tile(name, shape, dtype, tag=None):
+            return sb.tile(shape, dtype, name=name, tag=tag or name, align_bytes=64)
 
         def banks(name, tag):
             return [ps.tile([P, 2, SLOTS], F32, name=name + str(h), tag=tag + str(h)) for h in range(2)]
@@ -42,8 +42,8 @@ def tile_attend_bzcentred_asked_kernel(tc, query, query2, keys_words, keys_scale
         offsets = sb.tile([P, SLOTS // 16], U16, name="offsets")
         key_bytes = tile("key_bytes", [P, POOL], U8)
         tab_bytes = tile("tab_bytes", [P, POOL], U8)
-        nc.vector.memset(tab_bytes[:].bitcast(I32), 0)
-        nc.gpsimd.memset(key_bytes[:].bitcast(I32), 0)
+        nc.vector.memset(key_bytes[:].bitcast(I32), 0)
+        nc.gpsimd.memset(tab_bytes[:].bitcast(I32), 0)
         nc.sync.dma_start(offsets[:], offs)
 
         def load(name, src):
@@ -56,21 +56,24 @@ def tile_attend_bzcentred_asked_kernel(tc, query, query2, keys_words, keys_scale
                 nc.sync.dma_start(dst[32 * quad:32 * quad + 4, :].bitcast(I32),
                                   src[0, 4 * quad:4 * quad + 4, :].bitcast(I32))
 
-        tab_pool = tile("tab_pool", [P, POOL], U16)
-        nc.sync.dma_start(tab_pool[:].bitcast(I32), tab_words[0].bitcast(I32))
-        load_bytes(tab_bytes, tab_scales)
-        w1_raw = load("w1_raw", w1)
+        warm = tile("warm", [P, 4], F32)
+        nc.vector.memset(warm[:, 0:1], 0.0)
+        nc.scalar.activation(warm[:, 1:2], warm[:, 0:1], ACT.Sigmoid)
         key_words = tile("key_words", [P, POOL], U16)
         nc.sync.dma_start(key_words[:].bitcast(I32), keys_words[0].bitcast(I32))
         load_bytes(key_bytes, keys_scales)
+        tab_pool = tile("tab_pool", [P, POOL], U16)
+        nc.sync.dma_start(tab_pool[:].bitcast(I32), tab_words[0].bitcast(I32))
         q2_raw = load("q2_raw", query2)
+        load_bytes(tab_bytes, tab_scales)
         q_raw = load("q_raw", query)
-        share_sb = tile("share_sb", [P, PACK], F32)
-        nc.sync.dma_start(share_sb[:], share.rearrange("(p j) o -> p (j o)", j=PACK))
         qs_sb = tile("qs_sb", [P, PACK], F32)
         nc.sync.dma_start(qs_sb[:], qs.rearrange("(p j) o -> p (j o)", j=PACK))
+        share_sb = tile("share_sb", [P, PACK], F32)
+        nc.sync.dma_start(share_sb[:], share.rearrange("(p j) o -> p (j o)", j=PACK))
         sg_col = tile("sg_col", [P, 2], F32)
         nc.sync.dma_start(sg_col[:], sg.rearrange("o (p e) -> p (o e)", e=2))
+        w1_raw = load("w1_raw", w1)
         g_raw = load("g_raw", grows)
         old_sb = tile("old_sb", [P, PACK, SLOTS], F32)
         nc.sync.dma_start(old_sb[:], old.rearrange("(p j) i -> p j i", j=PACK))
@@ -78,15 +81,13 @@ def tile_attend_bzcentred_asked_kernel(tc, query, query2, keys_words, keys_scale
         make_identity(nc, ident[:])
         share16 = tile("share16", [P, PACK], F32)
         nc.gpsimd.tensor_scalar(share16[:], share_sb[:], 1.0 / PAGE, 0.0, ALU.mult, ALU.add)
-        warm2 = tile("warm2", [P, 1], F32)
-        nc.scalar.activation(warm2[:], ident[:, 0:1], ACT.Sigmoid)
         def gather(name, window, dtype):
             got = tile(name, [P, SLOTS], dtype)
             nc.vector.tensor_copy(got[:], window[:].indirect(offsets[:]))
             return got
 
-        def deal(name, raw, shares):
-            dealt = tile(name, [P, PACK, P, PACK], BF16)
+        def deal(name, raw, shares, tag=None):
+            dealt = tile(name, [P, PACK, P, PACK], BF16, tag)
             dst = dealt[:].rearrange("p r s t -> p s t r")
             src = raw[:].rearrange("p t (s r) -> p s t r", r=PACK)
             lo = 0
@@ -121,44 +122,29 @@ def tile_attend_bzcentred_asked_kernel(tc, query, query2, keys_words, keys_scale
         def spread(sums):
             return sums.unsqueeze(2).to_broadcast([P, PAGES, PAGE])
 
-        tabs = gather("tabs", tab_pool, U16)
-        tab_scale = gather("tab_scale", tab_bytes, U8)
-        w1_bf = deal("w1_bf", w1_raw, [("v", 72), ("s", 56)])
         keys = gather("keys", key_words, U16)
-        w1_mx = quantize("w1", w1_bf, WIDTH)
-        z_ps = banks("z_ps", "layer")
-        product(z_ps, w1_mx, tabs[:].bitcast(FP4X4), tab_scale[:])
         key_scale = gather("key_scale", key_bytes, U8)
-        q2_bf = deal("q2_bf", q2_raw, [("v", 72), ("s", 56)])
+        tabs = gather("tabs", tab_pool, U16)
+        q2_bf = deal("q2_bf", q2_raw, [("v", 88), ("s", 40)])
         q2_mx = quantize("q2", q2_bf, WIDTH)
         b_ps = banks("b_ps", "early")
         product(b_ps, q2_mx, keys[:].bitcast(FP4X4), key_scale[:])
         gate = tile("gate", [P, PACK, SLOTS], F32)
         for h in range(2):
             nc.scalar.activation(gate[:, 2 * h:2 * h + 2, :], b_ps[h][:], ACT.Sigmoid)
-        z_sum = tile("z_sum", [P, PACK, PAGES], F32)
-        for h in range(2):
-            nc.vector.tensor_reduce(z_sum[:, 2 * h:2 * h + 2, :],
-                                    z_ps[h][:].rearrange("p j (g m) -> p j g m", m=PAGE), AX.X, ALU.add)
+        nc.scalar.activation(warm[:, 2:3], gate[:, PACK - 1, SLOTS - 1:SLOTS], ACT.Exp)
+        tab_scale = gather("tab_scale", tab_bytes, U8)
         q_bf = deal("q_bf", q_raw, [("v", 128)])
         q_mx = quantize("q", q_bf, WIDTH)
         a_ps = banks("a_ps", "score")
         product(a_ps, q_mx, keys[:].bitcast(FP4X4), key_scale[:])
-        sg_ps = ps.tile([P, 2, P], F32, name="sg_ps", tag="sg")
-        for e in range(2):
-            nc.tensor.transpose(sg_ps[:, e, :], sg_col[:, e:e + 1].to_broadcast([P, P]), ident[:])
-
-        centred = tile("centred", [P, PACK, SLOTS], F32)
-        for j in range(PACK):
-            nc.vector.scalar_tensor_tensor(paged(centred[:, j, :]), spread(z_sum[:, j, :]), share16[:, j:j + 1],
-                                           paged(z_ps[j // 2][:, j % 2, :]), ALU.mult, ALU.subtract)
         neg_max = tile("neg_max", [P, PACK], F32)
         for h in range(2):
             nc.vector.tensor_reduce(neg_max[:, 2 * h:2 * h + 2], a_ps[h][:], AX.X, ALU.max, negate=True)
         expo = tile("expo", [P, PACK, SLOTS], F32)
         for t in range(PACK):
             nc.scalar.activation(expo[:, t, :], a_ps[t // 2][:, t % 2, :], ACT.Exp, bias=neg_max[:, t:t + 1])
-        g_bf = deal("g_bf", g_raw, [("s", 32), ("s", 32), ("s", 32), ("s", 32)])
+        w1_bf = deal("w1_bf", w1_raw, [("v", 48), ("s", 40), ("s", 40)])
         prob = tile("prob", [P, PACK, SLOTS], F32)
         row_sum = tile("row_sum", [P, PACK], F32)
         for t in range(PACK):
@@ -166,22 +152,38 @@ def tile_attend_bzcentred_asked_kernel(tc, query, query2, keys_words, keys_scale
                                            accum_out=row_sum[:, t:t + 1])
         inv_sum = tile("inv_sum", [P, PACK], F32)
         nc.vector.reciprocal(inv_sum[:], row_sum[:])
-        g_mx = quantize("g", g_bf, WIDTH)
         factor = tile("factor", [P, PACK], F32)
         nc.vector.tensor_tensor(factor[:], inv_sum[:], qs_sb[:], ALU.mult)
-        hv = tile("hv", [P, PACK, SLOTS], F32)
-        hv2 = tile("hv2", [P, PACK, SLOTS], F32)
-        for h in range(2):
-            nc.scalar.activation(hv[:, 2 * h:2 * h + 2, :], centred[:, 2 * h:2 * h + 2, :], ACT.Tanh)
-            nc.scalar.activation(hv2[:, 2 * h:2 * h + 2, :], hv[:, 2 * h:2 * h + 2, :], ACT.Square)
         wq_bf = tile("wq_bf", [P, SLOTS, PACK], BF16)
         nc.vector.tensor_tensor(
             wq_bf[:].rearrange("p (c i) t -> p c t i", i=4),
             prob[:].rearrange("p t (c i) -> p c t i", i=4),
             factor[:].unsqueeze(1).unsqueeze(3).to_broadcast([P, SLOTS // 4, PACK, 4]), ALU.mult)
         wq_codes, wq_scales = quantize("wq", wq_bf[:].rearrange("p i t -> p (i t)"), SLOTS)
+        w1_mx = quantize("w1", w1_bf, WIDTH)
+        z_ps = banks("z_ps", "layer")
+        product(z_ps, w1_mx, tabs[:].bitcast(FP4X4), tab_scale[:])
+        sg_ps = ps.tile([P, 2, P], F32, name="sg_ps", tag="sg")
+        for e in range(2):
+            nc.tensor.transpose(sg_ps[:, e, :], sg_col[:, e:e + 1].to_broadcast([P, P]), ident[:])
+
+        g_bf = deal("g_bf", g_raw, [("s", 32), ("s", 32), ("s", 32), ("s", 32)])
+        g_mx = quantize("g", g_bf, WIDTH)
         c_ps = banks("c_ps", "early")
         product(c_ps, g_mx, wq_codes[:].bitcast(FP8X4), wq_scales[:])
+        z_sum = tile("z_sum", [P, PACK, PAGES], F32)
+        centred = tile("centred", [P, PACK, SLOTS], F32)
+        hv = tile("hv", [P, PACK, SLOTS], F32)
+        hv2 = tile("hv2", [P, PACK, SLOTS], F32)
+        for h in range(2):
+            pair = slice(2 * h, 2 * h + 2)
+            nc.vector.tensor_reduce(z_sum[:, pair, :], z_ps[h][:].rearrange("p j (g m) -> p j g m", m=PAGE),
+                                    AX.X, ALU.add)
+            for j in range(2 * h, 2 * h + 2):
+                nc.vector.scalar_tensor_tensor(paged(centred[:, j, :]), spread(z_sum[:, j, :]), share16[:, j:j + 1],
+                                               paged(z_ps[h][:, j % 2, :]), ALU.mult, ALU.subtract)
+            nc.scalar.activation(hv[:, pair, :], centred[:, pair, :], ACT.Tanh)
+            nc.scalar.activation(hv2[:, pair, :], hv[:, pair, :], ACT.Square)
         neg_g = tile("neg_g", [P, PACK, SLOTS], F32)
         g_sum = tile("g_sum", [P, PACK, PAGES], F32)
         dzh = tile("dzh", [P, PACK, SLOTS], F32)
@@ -191,12 +193,8 @@ def tile_attend_bzcentred_asked_kernel(tc, query, query2, keys_words, keys_scale
         for h in range(2):
             pair = slice(2 * h, 2 * h + 2)
             nc.vector.scalar_tensor_tensor(neg_g[:, pair, :], hv2[:, pair, :], 1.0, c_ps[h][:], ALU.subtract, ALU.mult)
-        for h in range(2):
-            pair = slice(2 * h, 2 * h + 2)
             nc.vector.tensor_reduce(g_sum[:, pair, :], neg_g[:, pair, :].rearrange("p j (g m) -> p j g m", m=PAGE),
                                     AX.X, ALU.add)
-        for h in range(2):
-            pair = slice(2 * h, 2 * h + 2)
             for j in range(2 * h, 2 * h + 2):
                 nc.vector.scalar_tensor_tensor(paged(dzh[:, j, :]), spread(g_sum[:, j, :]), share16[:, j:j + 1],
                                                paged(neg_g[:, j, :]), ALU.mult, ALU.subtract)

@@ -42,8 +42,8 @@ def tile_attend_bzcentred_asked_kernel(tc, query, query2, keys_words, keys_scale
         offsets = sb.tile([P, SLOTS // 16], U16, name="offsets")
         key_bytes = tile("key_bytes", [P, POOL], U8)
         tab_bytes = tile("tab_bytes", [P, POOL], U8)
-        nc.vector.memset(key_bytes[:].bitcast(I32), 0)
-        nc.gpsimd.memset(tab_bytes[:].bitcast(I32), 0)
+        nc.vector.memset(tab_bytes[:].bitcast(I32), 0)
+        nc.gpsimd.memset(key_bytes[:].bitcast(I32), 0)
         nc.sync.dma_start(offsets[:], offs)
 
         def load(name, src):
@@ -59,21 +59,21 @@ def tile_attend_bzcentred_asked_kernel(tc, query, query2, keys_words, keys_scale
         warm = tile("warm", [P, 4], F32)
         nc.vector.memset(warm[:, 0:1], 0.0)
         nc.scalar.activation(warm[:, 1:2], warm[:, 0:1], ACT.Sigmoid)
-        key_words = tile("key_words", [P, POOL], U16)
-        nc.sync.dma_start(key_words[:].bitcast(I32), keys_words[0].bitcast(I32))
-        load_bytes(key_bytes, keys_scales)
         tab_pool = tile("tab_pool", [P, POOL], U16)
         nc.sync.dma_start(tab_pool[:].bitcast(I32), tab_words[0].bitcast(I32))
-        q2_raw = load("q2_raw", query2)
         load_bytes(tab_bytes, tab_scales)
-        q_raw = load("q_raw", query)
-        qs_sb = tile("qs_sb", [P, PACK], F32)
-        nc.sync.dma_start(qs_sb[:], qs.rearrange("(p j) o -> p (j o)", j=PACK))
+        key_words = tile("key_words", [P, POOL], U16)
+        nc.sync.dma_start(key_words[:].bitcast(I32), keys_words[0].bitcast(I32))
+        w1_raw = load("w1_raw", w1)
+        load_bytes(key_bytes, keys_scales)
+        q2_raw = load("q2_raw", query2)
         share_sb = tile("share_sb", [P, PACK], F32)
         nc.sync.dma_start(share_sb[:], share.rearrange("(p j) o -> p (j o)", j=PACK))
+        qs_sb = tile("qs_sb", [P, PACK], F32)
+        nc.sync.dma_start(qs_sb[:], qs.rearrange("(p j) o -> p (j o)", j=PACK))
         sg_col = tile("sg_col", [P, 2], F32)
         nc.sync.dma_start(sg_col[:], sg.rearrange("o (p e) -> p (o e)", e=2))
-        w1_raw = load("w1_raw", w1)
+        q_raw = load("q_raw", query)
         g_raw = load("g_raw", grows)
         old_sb = tile("old_sb", [P, PACK, SLOTS], F32)
         nc.sync.dma_start(old_sb[:], old.rearrange("(p j) i -> p j i", j=PACK))
@@ -122,9 +122,28 @@ def tile_attend_bzcentred_asked_kernel(tc, query, query2, keys_words, keys_scale
         def spread(sums):
             return sums.unsqueeze(2).to_broadcast([P, PAGES, PAGE])
 
-        keys = gather("keys", key_words, U16)
-        key_scale = gather("key_scale", key_bytes, U8)
         tabs = gather("tabs", tab_pool, U16)
+        tabs_split = tile("tabs_split", [P, SLOTS], U16)
+        nc.vector.tensor_copy(tabs_split[:].bitcast(I32).rearrange("p (u g w) -> p g u w", u=2, g=PAGES),
+                              tabs[:].bitcast(I32).rearrange("p (g u w) -> p g u w", u=2, g=PAGES))
+        tab_scale = gather("tab_scale", tab_bytes, U8)
+        tab_scale_split = tile("tab_scale_split", [P, SLOTS], U8)
+        nc.vector.tensor_copy(tab_scale_split[:].bitcast(I32).rearrange("p (u g w) -> p g u w", u=2, g=PAGES),
+                              tab_scale[:].bitcast(I32).rearrange("p (g u w) -> p g u w", u=2, g=PAGES))
+        keys = gather("keys", key_words, U16)
+        w1_bf = deal("w1_bf", w1_raw, [("v", 88), ("s", 40)])
+        w1_mx = quantize("w1", w1_bf, WIDTH)
+        pair_ps = ps.tile([P, PACK, P], F32, name="pair_ps", tag="pair")
+        for j in range(PACK):
+            cols = slice(P * j, P * (j + 1))
+            for u in range(2):
+                part = slice(P * u, P * (u + 1))
+                nc.tensor.matmul_mx(out=pair_ps[:, j, :], lhsT=w1_mx[0][:, cols].bitcast(FP8X4),
+                                    lhsT_scale=w1_mx[1][:, cols], rhs=tabs_split[:, part].bitcast(FP4X4),
+                                    rhs_scale=tab_scale_split[:, part], start=(u == 0), stop=(u == 1))
+        z_ps = banks("z_ps", "layer")
+        product(z_ps, w1_mx, tabs[:].bitcast(FP4X4), tab_scale[:])
+        key_scale = gather("key_scale", key_bytes, U8)
         q2_bf = deal("q2_bf", q2_raw, [("v", 88), ("s", 40)])
         q2_mx = quantize("q2", q2_bf, WIDTH)
         b_ps = banks("b_ps", "early")
@@ -133,7 +152,12 @@ def tile_attend_bzcentred_asked_kernel(tc, query, query2, keys_words, keys_scale
         for h in range(2):
             nc.scalar.activation(gate[:, 2 * h:2 * h + 2, :], b_ps[h][:], ACT.Sigmoid)
         nc.scalar.activation(warm[:, 2:3], gate[:, PACK - 1, SLOTS - 1:SLOTS], ACT.Exp)
-        tab_scale = gather("tab_scale", tab_bytes, U8)
+        sg_ps = ps.tile([P, 2, P], F32, name="sg_ps", tag="sg")
+        for e in range(2):
+            nc.tensor.transpose(sg_ps[:, e, :], sg_col[:, e:e + 1].to_broadcast([P, P]), ident[:])
+
+        z_sum = tile("z_sum", [P, PACK, PAGES], F32, "q2_bf")
+        nc.vector.tensor_reduce(z_sum[:], pair_ps[:].rearrange("p j (g m) -> p j g m", m=PAGE // 2), AX.X, ALU.add)
         q_bf = deal("q_bf", q_raw, [("v", 128)])
         q_mx = quantize("q", q_bf, WIDTH)
         a_ps = banks("a_ps", "score")
@@ -144,7 +168,7 @@ def tile_attend_bzcentred_asked_kernel(tc, query, query2, keys_words, keys_scale
         expo = tile("expo", [P, PACK, SLOTS], F32)
         for t in range(PACK):
             nc.scalar.activation(expo[:, t, :], a_ps[t // 2][:, t % 2, :], ACT.Exp, bias=neg_max[:, t:t + 1])
-        w1_bf = deal("w1_bf", w1_raw, [("v", 48), ("s", 40), ("s", 40)])
+        g_bf = deal("g_bf", g_raw, [("s", 128)], "neg_max")
         prob = tile("prob", [P, PACK, SLOTS], F32)
         row_sum = tile("row_sum", [P, PACK], F32)
         for t in range(PACK):
@@ -154,36 +178,35 @@ def tile_attend_bzcentred_asked_kernel(tc, query, query2, keys_words, keys_scale
         nc.vector.reciprocal(inv_sum[:], row_sum[:])
         factor = tile("factor", [P, PACK], F32)
         nc.vector.tensor_tensor(factor[:], inv_sum[:], qs_sb[:], ALU.mult)
+        hv = tile("hv", [P, PACK, SLOTS], F32)
+        hv2 = tile("hv2", [P, PACK, SLOTS], F32)
+        centred = tile("centred0", [P, 2, SLOTS], F32, "q_bf")
+        for j in range(0, 2):
+            nc.vector.scalar_tensor_tensor(paged(centred[:, j % 2, :]), spread(z_sum[:, j, :]), share16[:, j:j + 1],
+                                           paged(z_ps[0][:, j % 2, :]), ALU.mult, ALU.subtract)
+        nc.scalar.activation(hv[:, 0:2, :], centred[:], ACT.Tanh)
+        nc.scalar.activation(hv2[:, 0:2, :], hv[:, 0:2, :], ACT.Square)
+        centred = tile("centred1", [P, 2, SLOTS], F32, "gate")
+        for j in range(2, 4):
+            nc.vector.scalar_tensor_tensor(paged(centred[:, j % 2, :]), spread(z_sum[:, j, :]), share16[:, j:j + 1],
+                                           paged(z_ps[1][:, j % 2, :]), ALU.mult, ALU.subtract)
+        nc.scalar.activation(hv[:, 2:4, :], centred[:], ACT.Tanh)
+        nc.scalar.activation(hv2[:, 2:4, :], hv[:, 2:4, :], ACT.Square)
         wq_bf = tile("wq_bf", [P, SLOTS, PACK], BF16)
         nc.vector.tensor_tensor(
             wq_bf[:].rearrange("p (c i) t -> p c t i", i=4),
             prob[:].rearrange("p t (c i) -> p c t i", i=4),
             factor[:].unsqueeze(1).unsqueeze(3).to_broadcast([P, SLOTS // 4, PACK, 4]), ALU.mult)
+        g_lo = quantize("g_lo", g_bf[:, :2 * WIDTH], WIDTH // 2)
         wq_codes, wq_scales = quantize("wq", wq_bf[:].rearrange("p i t -> p (i t)"), SLOTS)
-        w1_mx = quantize("w1", w1_bf, WIDTH)
-        z_ps = banks("z_ps", "layer")
-        product(z_ps, w1_mx, tabs[:].bitcast(FP4X4), tab_scale[:])
-        sg_ps = ps.tile([P, 2, P], F32, name="sg_ps", tag="sg")
-        for e in range(2):
-            nc.tensor.transpose(sg_ps[:, e, :], sg_col[:, e:e + 1].to_broadcast([P, P]), ident[:])
-
-        g_bf = deal("g_bf", g_raw, [("s", 32), ("s", 32), ("s", 32), ("s", 32)])
-        g_mx = quantize("g", g_bf, WIDTH)
+        g_hi = quantize("g_hi", g_bf[:, 2 * WIDTH:], WIDTH // 2)
         c_ps = banks("c_ps", "early")
-        product(c_ps, g_mx, wq_codes[:].bitcast(FP8X4), wq_scales[:])
-        z_sum = tile("z_sum", [P, PACK, PAGES], F32)
-        centred = tile("centred", [P, PACK, SLOTS], F32)
-        hv = tile("hv", [P, PACK, SLOTS], F32)
-        hv2 = tile("hv2", [P, PACK, SLOTS], F32)
-        for h in range(2):
-            pair = slice(2 * h, 2 * h + 2)
-            nc.vector.tensor_reduce(z_sum[:, pair, :], z_ps[h][:].rearrange("p j (g m) -> p j g m", m=PAGE),
-                                    AX.X, ALU.add)
-            for j in range(2 * h, 2 * h + 2):
-                nc.vector.scalar_tensor_tensor(paged(centred[:, j, :]), spread(z_sum[:, j, :]), share16[:, j:j + 1],
-                                               paged(z_ps[h][:, j % 2, :]), ALU.mult, ALU.subtract)
-            nc.scalar.activation(hv[:, pair, :], centred[:, pair, :], ACT.Tanh)
-            nc.scalar.activation(hv2[:, pair, :], hv[:, pair, :], ACT.Square)
+        for j in range(PACK):
+            codes, scales = (g_lo, g_hi)[j // 2]
+            cols = slice(P * (j % 2), P * (j % 2 + 1))
+            nc.tensor.matmul_mx(out=c_ps[j // 2][:, j % 2, :], lhsT=codes[:, cols].bitcast(FP8X4),
+                                lhsT_scale=scales[:, cols], rhs=wq_codes[:].bitcast(FP8X4), rhs_scale=wq_scales[:],
+                                start=True, stop=True)
         neg_g = tile("neg_g", [P, PACK, SLOTS], F32)
         g_sum = tile("g_sum", [P, PACK, PAGES], F32)
         dzh = tile("dzh", [P, PACK, SLOTS], F32)
@@ -202,5 +225,10 @@ def tile_attend_bzcentred_asked_kernel(tc, query, query2, keys_words, keys_scale
                 gained[:, pair, :].rearrange("p j (k e) -> p j k e", e=2),
                 dzh[:, pair, :].rearrange("p j (k e) -> p j k e", e=2),
                 sg_ps[:].rearrange("p e k -> p k e").unsqueeze(1).to_broadcast([P, 2, P, 2]), ALU.mult)
-            (nc.gpsimd if h == 0 else nc.vector).tensor_tensor(result[:, pair, :], gained[:, pair, :], old_sb[:, pair, :], ALU.add)
-            nc.sync.dma_start(out_v[:, pair, :], result[:, pair, :])
+            if h == 0:
+                nc.vector.tensor_tensor(result[:, pair, :], gained[:, pair, :], old_sb[:, pair, :], ALU.add)
+                nc.sync.dma_start(out_v[:, pair, :], result[:, pair, :])
+            else:
+                for j in range(2 * h, 2 * h + 2):
+                    nc.vector.tensor_tensor(result[:, j, :], gained[:, j, :], old_sb[:, j, :], ALU.add)
+                    nc.sync.dma_start(out_v[:, j, :], result[:, j, :])

from contextlib import ExitStack

import concourse.mybir as mybir
from concourse.masks import make_identity

F32 = mybir.dt.float32
BF16 = mybir.dt.bfloat16
I32 = mybir.dt.int32
U32 = mybir.dt.uint32
U16 = mybir.dt.uint16
U8 = mybir.dt.uint8
FP8X4 = mybir.dt.float8_e4m3fn_x4
FP4X4 = mybir.dt.float4_e2m1fn_x4
ALU = mybir.AluOpType
ACT = mybir.ActivationFunctionType
AX = mybir.AxisListType

P = 128
PACK = 4
WIDTH = 512
POOL = 1024
SLOTS = 256
PAGE = 16
PAGES = SLOTS // PAGE

FLOPS = 4 * 2 * 512 * 512 * SLOTS


def tile_attend_bzcentred_asked_kernel(tc, query, query2, keys_words, keys_scales, tab_words, tab_scales,
                                        w1, share, qs, grows, sg, old, offs, out):
    nc = tc.nc
    with ExitStack() as ctx:
        sb = ctx.enter_context(tc.tile_pool(name="sb", bufs=1))
        ps = ctx.enter_context(tc.psum_pool(name="ps", bufs=1))

        def tile(name, shape, dtype, tag=None):
            return sb.tile(shape, dtype, name=name, tag=tag or name, align_bytes=64)

        def banks(name, tag):
            return [ps.tile([P, 2, SLOTS], F32, name=name + str(h), tag=tag + str(h)) for h in range(2)]

        offsets = sb.tile([P, SLOTS // 16], U16, name="offsets")
        key_bytes = tile("key_bytes", [P, POOL], U8)
        tab_bytes = tile("tab_bytes", [P, POOL], U8)
        nc.vector.memset(tab_bytes[:].bitcast(I32), 0)
        nc.gpsimd.memset(key_bytes[:].bitcast(I32), 0)
        nc.sync.dma_start(offsets[:], offs)

        def load(name, src):
            raw = tile(name, [P, PACK, WIDTH], F32)
            nc.sync.dma_start(raw[:], src.rearrange("(p t) c -> p t c", t=PACK))
            return raw

        def load_bytes(dst, src):
            for quad in range(4):
                nc.sync.dma_start(dst[32 * quad:32 * quad + 4, :].bitcast(I32),
                                  src[0, 4 * quad:4 * quad + 4, :].bitcast(I32))

        warm = tile("warm", [P, 4], F32)
        nc.vector.memset(warm[:, 0:1], 0.0)
        nc.scalar.activation(warm[:, 1:2], warm[:, 0:1], ACT.Sigmoid)
        tab_pool = tile("tab_pool", [P, POOL], U16)
        nc.sync.dma_start(tab_pool[:].bitcast(I32), tab_words[0].bitcast(I32))
        load_bytes(tab_bytes, tab_scales)
        key_words = tile("key_words", [P, POOL], U16)
        nc.sync.dma_start(key_words[:].bitcast(I32), keys_words[0].bitcast(I32))
        w1_raw = load("w1_raw", w1)
        load_bytes(key_bytes, keys_scales)
        q2_raw = load("q2_raw", query2)
        share_sb = tile("share_sb", [P, PACK], F32)
        nc.sync.dma_start(share_sb[:], share.rearrange("(p j) o -> p (j o)", j=PACK))
        qs_sb = tile("qs_sb", [P, PACK], F32)
        nc.sync.dma_start(qs_sb[:], qs.rearrange("(p j) o -> p (j o)", j=PACK))
        sg_col = tile("sg_col", [P, 2], F32)
        nc.sync.dma_start(sg_col[:], sg.rearrange("o (p e) -> p (o e)", e=2))
        q_raw = load("q_raw", query)
        g_raw = load("g_raw", grows)
        old_sb = tile("old_sb", [P, PACK, SLOTS], F32)
        nc.sync.dma_start(old_sb[:], old.rearrange("(p j) i -> p j i", j=PACK))
        ident = tile("ident", [P, P], F32)
        make_identity(nc, ident[:])
        share16 = tile("share16", [P, PACK], F32)
        nc.gpsimd.tensor_scalar(share16[:], share_sb[:], 1.0 / PAGE, 0.0, ALU.mult, ALU.add)
        def gather(name, window, dtype):
            got = tile(name, [P, SLOTS], dtype)
            nc.vector.tensor_copy(got[:], window[:].indirect(offsets[:]))
            return got

        def deal(name, raw, shares, tag=None):
            dealt = tile(name, [P, PACK, P, PACK], BF16, tag)
            dst = dealt[:].rearrange("p r s t -> p s t r")
            src = raw[:].rearrange("p t (s r) -> p s t r", r=PACK)
            lo = 0
            for engine, cols in shares:
                part = slice(lo, lo + cols)
                if engine == "v":
                    nc.vector.tensor_copy(dst[:, part], src[:, part])
                elif engine == "s":
                    nc.scalar.copy(dst[:, part], src[:, part])
                else:
                    nc.gpsimd.tensor_scalar(dst[:, part], src[:, part], 1.0, 0.0, ALU.mult, ALU.add)
                lo = lo + cols
            return dealt[:].rearrange("p r s t -> p (r s t)")

        def quantize(name, values, width):
            codes = tile(name + "_codes", [P, width], U32)
            scales = tile(name + "_scales", [P, width], U8)
            nc.vector.quantize_mx(out=codes[:].bitcast(FP8X4), scales=scales[:], in_=values)
            return codes, scales

        def product(dst, stationary, moving_codes, moving_scales):
            codes, scales = stationary
            for r in range(PACK):
                cols = slice(P * r, P * (r + 1))
                nc.tensor.matmul_mx(out=dst[r // 2][:, r % 2, :], lhsT=codes[:, cols].bitcast(FP8X4),
                                    lhsT_scale=scales[:, cols], rhs=moving_codes, rhs_scale=moving_scales,
                                    start=True, stop=True)

        def paged(ap):
            return ap.rearrange("p (g m) -> p g m", m=PAGE)

        def spread(sums):
            return sums.unsqueeze(2).to_broadcast([P, PAGES, PAGE])

        tabs = gather("tabs", tab_pool, U16)
        tabs_split = tile("tabs_split", [P, SLOTS], U16)
        nc.vector.tensor_copy(tabs_split[:].bitcast(I32).rearrange("p (u g w) -> p g u w", u=2, g=PAGES),
                              tabs[:].bitcast(I32).rearrange("p (g u w) -> p g u w", u=2, g=PAGES))
        tab_scale = gather("tab_scale", tab_bytes, U8)
        tab_scale_split = tile("tab_scale_split", [P, SLOTS], U8)
        nc.vector.tensor_copy(tab_scale_split[:].bitcast(I32).rearrange("p (u g w) -> p g u w", u=2, g=PAGES),
                              tab_scale[:].bitcast(I32).rearrange("p (g u w) -> p g u w", u=2, g=PAGES))
        keys = gather("keys", key_words, U16)
        w1_bf = deal("w1_bf", w1_raw, [("v", 88), ("s", 40)])
        w1_mx = quantize("w1", w1_bf, WIDTH)
        pair_ps = ps.tile([P, PACK, P], F32, name="pair_ps", tag="pair")
        for j in range(PACK):
            cols = slice(P * j, P * (j + 1))
            for u in range(2):
                part = slice(P * u, P * (u + 1))
                nc.tensor.matmul_mx(out=pair_ps[:, j, :], lhsT=w1_mx[0][:, cols].bitcast(FP8X4),
                                    lhsT_scale=w1_mx[1][:, cols], rhs=tabs_split[:, part].bitcast(FP4X4),
                                    rhs_scale=tab_scale_split[:, part], start=(u == 0), stop=(u == 1))
        z_ps = banks("z_ps", "layer")
        product(z_ps, w1_mx, tabs[:].bitcast(FP4X4), tab_scale[:])
        key_scale = gather("key_scale", key_bytes, U8)
        q2_bf = deal("q2_bf", q2_raw, [("v", 88), ("s", 40)])
        q2_mx = quantize("q2", q2_bf, WIDTH)
        b_ps = banks("b_ps", "early")
        product(b_ps, q2_mx, keys[:].bitcast(FP4X4), key_scale[:])
        gate = tile("gate", [P, PACK, SLOTS], F32)
        for h in range(2):
            nc.scalar.activation(gate[:, 2 * h:2 * h + 2, :], b_ps[h][:], ACT.Sigmoid)
        nc.scalar.activation(warm[:, 2:3], gate[:, PACK - 1, SLOTS - 1:SLOTS], ACT.Exp)
        sg_ps = ps.tile([P, 2, P], F32, name="sg_ps", tag="sg")
        for e in range(2):
            nc.tensor.transpose(sg_ps[:, e, :], sg_col[:, e:e + 1].to_broadcast([P, P]), ident[:])

        z_sum = tile("z_sum", [P, PACK, PAGES], F32, "q2_bf")
        nc.vector.tensor_reduce(z_sum[:], pair_ps[:].rearrange("p j (g m) -> p j g m", m=PAGE // 2), AX.X, ALU.add)
        q_bf = deal("q_bf", q_raw, [("v", 128)])
        q_mx = quantize("q", q_bf, WIDTH)
        a_ps = banks("a_ps", "score")
        product(a_ps, q_mx, keys[:].bitcast(FP4X4), key_scale[:])
        neg_max = tile("neg_max", [P, PACK], F32)
        for h in range(2):
            nc.vector.tensor_reduce(neg_max[:, 2 * h:2 * h + 2], a_ps[h][:], AX.X, ALU.max, negate=True)
        expo = tile("expo", [P, PACK, SLOTS], F32)
        for t in range(PACK):
            nc.scalar.activation(expo[:, t, :], a_ps[t // 2][:, t % 2, :], ACT.Exp, bias=neg_max[:, t:t + 1])
        g_bf = deal("g_bf", g_raw, [("s", 128)], "neg_max")
        prob = tile("prob", [P, PACK, SLOTS], F32)
        row_sum = tile("row_sum", [P, PACK], F32)
        for t in range(PACK):
            nc.vector.scalar_tensor_tensor(prob[:, t, :], expo[:, t, :], 1.0, gate[:, t, :], ALU.mult, ALU.mult,
                                           accum_out=row_sum[:, t:t + 1])
        inv_sum = tile("inv_sum", [P, PACK], F32)
        nc.vector.reciprocal(inv_sum[:], row_sum[:])
        factor = tile("factor", [P, PACK], F32)
        nc.vector.tensor_tensor(factor[:], inv_sum[:], qs_sb[:], ALU.mult)
        hv = tile("hv", [P, PACK, SLOTS], F32)
        hv2 = tile("hv2", [P, PACK, SLOTS], F32)
        centred = tile("centred0", [P, 2, SLOTS], F32, "q_bf")
        for j in range(0, 2):
            nc.vector.scalar_tensor_tensor(paged(centred[:, j % 2, :]), spread(z_sum[:, j, :]), share16[:, j:j + 1],
                                           paged(z_ps[0][:, j % 2, :]), ALU.mult, ALU.subtract)
        nc.scalar.activation(hv[:, 0:2, :], centred[:], ACT.Tanh)
        nc.scalar.activation(hv2[:, 0:2, :], hv[:, 0:2, :], ACT.Square)
        centred = tile("centred1", [P, 2, SLOTS], F32, "gate")
        for j in range(2, 4):
            nc.vector.scalar_tensor_tensor(paged(centred[:, j % 2, :]), spread(z_sum[:, j, :]), share16[:, j:j + 1],
                                           paged(z_ps[1][:, j % 2, :]), ALU.mult, ALU.subtract)
        nc.scalar.activation(hv[:, 2:4, :], centred[:], ACT.Tanh)
        nc.scalar.activation(hv2[:, 2:4, :], hv[:, 2:4, :], ACT.Square)
        wq_bf = tile("wq_bf", [P, SLOTS, PACK], BF16)
        nc.vector.tensor_tensor(
            wq_bf[:].rearrange("p (c i) t -> p c t i", i=4),
            prob[:].rearrange("p t (c i) -> p c t i", i=4),
            factor[:].unsqueeze(1).unsqueeze(3).to_broadcast([P, SLOTS // 4, PACK, 4]), ALU.mult)
        g_lo = quantize("g_lo", g_bf[:, :2 * WIDTH], WIDTH // 2)
        wq_codes, wq_scales = quantize("wq", wq_bf[:].rearrange("p i t -> p (i t)"), SLOTS)
        g_hi = quantize("g_hi", g_bf[:, 2 * WIDTH:], WIDTH // 2)
        c_ps = banks("c_ps", "early")
        for j in range(PACK):
            codes, scales = (g_lo, g_hi)[j // 2]
            cols = slice(P * (j % 2), P * (j % 2 + 1))
            nc.tensor.matmul_mx(out=c_ps[j // 2][:, j % 2, :], lhsT=codes[:, cols].bitcast(FP8X4),
                                lhsT_scale=scales[:, cols], rhs=wq_codes[:].bitcast(FP8X4), rhs_scale=wq_scales[:],
                                start=True, stop=True)
        neg_g = tile("neg_g", [P, PACK, SLOTS], F32)
        g_sum = tile("g_sum", [P, PACK, PAGES], F32)
        dzh = tile("dzh", [P, PACK, SLOTS], F32)
        gained = tile("gained", [P, PACK, SLOTS], F32)
        result = tile("result", [P, PACK, SLOTS], F32)
        out_v = out.rearrange("(p j) i -> p j i", j=PACK)
        for h in range(2):
            pair = slice(2 * h, 2 * h + 2)
            nc.vector.scalar_tensor_tensor(neg_g[:, pair, :], hv2[:, pair, :], 1.0, c_ps[h][:], ALU.subtract, ALU.mult)
            nc.vector.tensor_reduce(g_sum[:, pair, :], neg_g[:, pair, :].rearrange("p j (g m) -> p j g m", m=PAGE),
                                    AX.X, ALU.add)
            for j in range(2 * h, 2 * h + 2):
                nc.vector.scalar_tensor_tensor(paged(dzh[:, j, :]), spread(g_sum[:, j, :]), share16[:, j:j + 1],
                                               paged(neg_g[:, j, :]), ALU.mult, ALU.subtract)
            nc.vector.tensor_tensor(
                gained[:, pair, :].rearrange("p j (k e) -> p j k e", e=2),
                dzh[:, pair, :].rearrange("p j (k e) -> p j k e", e=2),
                sg_ps[:].rearrange("p e k -> p k e").unsqueeze(1).to_broadcast([P, 2, P, 2]), ALU.mult)
            if h == 0:
                nc.vector.tensor_tensor(result[:, pair, :], gained[:, pair, :], old_sb[:, pair, :], ALU.add)
                nc.sync.dma_start(out_v[:, pair, :], result[:, pair, :])
            else:
                for j in range(2 * h, 2 * h + 2):
                    nc.vector.tensor_tensor(result[:, j, :], gained[:, j, :], old_sb[:, j, :], ALU.add)
                    nc.sync.dma_start(out_v[:, j, :], result[:, j, :])
